import numpy as np
import ml_dtypes


def mxq(x, axis, fmt="e4m3"):
    dtype, down = {"e4m3": (ml_dtypes.float8_e4m3fn, 7), "e5m2": (ml_dtypes.float8_e5m2, 14)}[fmt]
    v = np.moveaxis(np.asarray(x, np.float32).astype(ml_dtypes.bfloat16).astype(np.float64), axis, -1)
    blocks = v.reshape(v.shape[:-1] + (-1, 32))
    amax = np.abs(blocks).max(-1, keepdims=True)
    byte = np.maximum(np.where(amax > 0, np.frexp(amax)[1] - 1 + 127, 0) - down, 1)
    scale = np.exp2(byte - 127.0)
    codes = (blocks / scale).astype(np.float32).astype(dtype).astype(np.float64)
    return np.moveaxis((codes * scale).reshape(v.shape), -1, axis)


WIDE = False


def mx_kscale(k):
    if not WIDE:
        return np.ones(k)
    levels = np.array([10, -10, 5, -5, 0])
    if k % 512:
        return np.exp2(np.random.permutation(np.resize(levels, k // 32))).repeat(32)
    a = np.empty((k // 512, 16))
    for p in range(k // 512):
        a[p, :8] = np.random.permutation(np.resize(levels, 8))
        for g in range(8):
            far = levels[np.abs(levels - a[p, g]) >= 10]
            a[p, g + 8] = far[np.random.randint(len(far))]
    return np.exp2(a.ravel()).repeat(32)


BF16 = ml_dtypes.bfloat16


def bf(x):
    return np.asarray(x, np.float32).astype(BF16)


def f64(x):
    return np.asarray(x).astype(np.float64)


E2M1 = np.array([0.0, 0.5, 1.0, 1.5, 2.0, 3.0, 4.0, 6.0, -0.0, -0.5, -1.0, -1.5, -2.0, -3.0, -4.0, -6.0])


def pack_weight(w, fmt):
    k, n = w.shape
    w = f64(bf(w)).reshape(k // 32, 32, n)
    amax = np.abs(w).max(1)
    if fmt == "e4m3":
        byte = np.frexp(amax)[1] - 1 + 127 - 7
    else:
        mant, ex = np.frexp(amax / 6.0)
        byte = np.where(mant > 0.5, ex, ex - 1) + 127
    byte = np.clip(np.where(amax > 0, byte, 1), 1, 254)
    scaled = (w * np.exp2(127.0 - byte)[:, None, :]).reshape(k, n).astype(np.float32)
    by_word = np.ascontiguousarray(scaled.reshape(k // 512, 128, 4, n).transpose(0, 1, 3, 2))
    if fmt == "e4m3":
        words = by_word.astype(ml_dtypes.float8_e4m3fn).view(np.uint8)
    else:
        c = by_word.astype(ml_dtypes.float4_e2m1fn).view(np.uint8) & 0xF
        words = c[..., 0::2] | (c[..., 1::2] << 4)
    return np.ascontiguousarray(words), np.ascontiguousarray(byte.astype(np.uint8).reshape(k // 512, 16, n))


def unpack_weight(words, scales, fmt):
    g, p, n, _ = words.shape
    if fmt == "e4m3":
        vals = np.ascontiguousarray(words).view(ml_dtypes.float8_e4m3fn).astype(np.float64)
    else:
        nib = np.empty((g, p, n, 4), np.uint8)
        nib[..., 0::2] = words & 0xF
        nib[..., 1::2] = words >> 4
        vals = E2M1[nib]
    vals = vals * np.repeat(np.exp2(scales.astype(np.float64) - 127.0), 8, axis=1)[..., None]
    return vals.transpose(0, 1, 3, 2).reshape(g * 512, n)
def pack4(w):
    words, scales = pack_weight(w, "e2m1")
    return words.reshape(words.shape[0], 128, -1), scales


def unpack4(words, scales):
    return unpack_weight(words.reshape(words.shape[0], 128, -1, 2), scales, "e2m1")


def planes(Y):
    n, m = Y.shape
    b = f64(bf(Y)).reshape(n // 32, 32, m)
    amax = np.abs(b).max(1)
    byte = np.clip(np.where(amax > 0, np.frexp(amax)[1] - 1 + 127 - 7, 1), 1, 254)
    codes = (b * np.exp2(127.0 - byte)[:, None, :]).reshape(n, m).astype(np.float32).astype(ml_dtypes.float8_e4m3fn).view(np.uint8)
    words = codes.reshape(n // 512, 128, 4, m).transpose(0, 1, 3, 2)
    return np.ascontiguousarray(words), np.ascontiguousarray(byte.astype(np.uint8).reshape(n // 512, 16, m))


G, N, C = 3, 512, 512


def so3_bracket(a, b):
    z0 = a[1] * b[2] - a[2] * b[1]
    z1 = a[2] * b[0] - a[0] * b[2]
    z2 = a[0] * b[1] - a[1] * b[0]
    return np.stack([z0, z1, z2], axis=0)


def setup_inputs():
    s, t = mx_kscale(C), mx_kscale(C)
    scale = 1.0 / np.sqrt(C)
    x = bf(np.random.standard_normal((G, N, C)) * s)
    u_words, u_scales = pack4(np.random.standard_normal((C, C)) * scale / s[:, None] * t)
    v_words, v_scales = pack4(np.random.standard_normal((C, C)) * scale / s[:, None])
    w_words, w_scales = pack4(np.random.standard_normal((C, C)) * scale / t[:, None])
    return {"x": x,
            "u_words": u_words, "u_scales": u_scales,
            "v_words": v_words, "v_scales": v_scales,
            "w_words": w_words, "w_scales": w_scales,
            "r": bf((1.0 + 0.1 * np.random.standard_normal(C)) / s)}


def core(x, u_words, u_scales, v_words, v_scales, w_words, w_scales, r):
    xq = mxq(f64(x), 2, "e4m3")
    a = xq @ unpack4(u_words, u_scales)
    b = xq @ unpack4(v_words, v_scales)
    z = so3_bracket(a, b)
    m = mxq(z, 2, "e4m3") @ unpack4(w_words, w_scales)
    y = f64(x) * f64(r)[None, None, :] + m
    return y


def reference(x, u_words, u_scales, v_words, v_scales, w_words, w_scales, r):
    R_out = core(x, u_words, u_scales, v_words, v_scales, w_words, w_scales, r)
    words, scales = planes(np.moveaxis(R_out, 2, 0).reshape(512, -1))
    return R_out, words, scales

@@ -1,0 +1,306 @@
+from contextlib import ExitStack
+
+import concourse.mybir as mybir
+from concourse.masks import make_identity
+
+F32 = mybir.dt.float32
+BF16 = mybir.dt.bfloat16
+I32 = mybir.dt.int32
+U32 = mybir.dt.uint32
+U8 = mybir.dt.uint8
+FP8X4 = mybir.dt.float8_e4m3fn_x4
+FP4X4 = mybir.dt.float4_e2m1fn_x4
+ALU = mybir.AluOpType
+
+G, N, C = 3, 512, 512
+P = 128
+PACK = 4
+TOK = 128
+CHUNKS = N // TOK
+FLOPS = 2 * 3 * G * N * C * C
+
+
+def tile_so3liebracketchannelmixer_x2_kernel(
+    tc, x, u_words, u_scales, v_words, v_scales, w_words, w_scales, r, out_0, out_1, out_2
+):
+    nc = tc.nc
+    with ExitStack() as ctx:
+        keep = ctx.enter_context(tc.tile_pool(name="keep", bufs=1))
+        work = ctx.enter_context(tc.tile_pool(name="work", bufs=2))
+        psum = ctx.enter_context(tc.psum_pool(name="psum", bufs=2))
+
+        out_words = out_1[0].rearrange("p m t -> p (m t)").bitcast(I32).rearrange("p (g m) -> p g m", g=G)
+        out_scales = out_2[0].bitcast(I32).rearrange("q (g m) -> q g m", g=G)
+
+        raw_words = [keep.tile([P, 2 * C], U8, name=f"raw_words{i}", align_bytes=64) for i in range(3)]
+        raw_scales = [keep.tile([P, C], U8, name=f"raw_scales{i}", align_bytes=64) for i in range(3)]
+        words = [keep.tile([P, 2 * C], U8, name=f"words{i}", align_bytes=64) for i in range(3)]
+        scales = [keep.tile([P, C], U8, name=f"scales{i}", align_bytes=64) for i in range(3)]
+        x_rows = [keep.tile([TOK, G, C], BF16, name=f"x_rows{c}", align_bytes=64) for c in range(CHUNKS)]
+        xt = [keep.tile([P, G * TOK * PACK], BF16, name=f"xt{c}", align_bytes=64) for c in range(CHUNKS)]
+        ident = keep.tile([P, P], F32, name="ident")
+        r_bf = keep.tile([P, PACK], BF16, name="r_bf")
+        r_col = keep.tile([P, PACK], F32, name="r_col")
+        y_scales_body = keep.tile([P, G, N - TOK], U8, name="y_scales_body", align_bytes=64)
+        y_scales_tail = keep.tile([P, G, TOK], U8, name="y_scales_tail", align_bytes=64)
+
+        xq, xs, bs, z, zq, zs, yt, y16, yq, m_ps, a_ps = {}, {}, {}, {}, {}, {}, {}, {}, {}, {}, {}
+
+        def load_x(c):
+            nc.sync.dma_start(out=x_rows[c][:], in_=x[:, c * TOK : (c + 1) * TOK, :].rearrange("g n c -> n g c"))
+
+        def load_words(i, src):
+            nc.sync.dma_start(out=raw_words[i][:].bitcast(I32), in_=src[0].bitcast(I32))
+
+        def load_scales(i, src, queue):
+            for q in range(4):
+                queue.dma_start(
+                    out=raw_scales[i][32 * q : 32 * q + 4, :].bitcast(I32),
+                    in_=src[0][4 * q : 4 * q + 4, :].bitcast(I32),
+                )
+
+        def permute_words(i):
+            nc.vector.tensor_copy(
+                out=words[i][:].rearrange("p (t m b) -> p t m b", t=PACK, b=2),
+                in_=raw_words[i][:].rearrange("p (m t b) -> p t m b", t=PACK, b=2),
+            )
+
+        def permute_scales(i):
+            nc.vector.tensor_copy(
+                out=scales[i][:].rearrange("p (t m) -> p t m", t=PACK),
+                in_=raw_scales[i][:].rearrange("p (m t) -> p t m", t=PACK),
+            )
+
+        def turn_x(c):
+            rows = x_rows[c][:].rearrange("n g c -> n (g c)").bitcast(F32)
+            dst = xt[c][:].bitcast(F32)
+            for g0, gn in ((0, 2), (2, 1)):
+                bank = psum.tile([P, 2, 2, TOK], F32, tag="turn", name="turn_x")
+                for g in range(gn):
+                    for h in range(2):
+                        lo = (g0 + g) * (C // 2)
+                        nc.tensor.transpose(bank[:, g, h, :], rows[:, lo + h : lo + C // 2 : 2], ident[:])
+                w = 2 * TOK
+                nc.scalar.copy(
+                    out=dst[:, g0 * w : (g0 + gn) * w].rearrange("p (g n h) -> p g n h", g=gn, h=2),
+                    in_=bank[:, 0:gn].rearrange("p g h n -> p g n h"),
+                )
+
+        def quant_x(c):
+            codes = work.tile([P, G * TOK], U32, name="xq", align_bytes=64)
+            sc = work.tile([P, G * TOK], U8, name="xs", align_bytes=64)
+            xq[c], xs[c] = codes, sc
+            for lo, hi in ((0, 2), (2, 3)):
+                nc.vector.quantize_mx(
+                    out=codes[:, lo * TOK : hi * TOK].bitcast(FP8X4),
+                    scales=sc[:, lo * TOK : hi * TOK],
+                    in_=xt[c][:, lo * TOK * PACK : hi * TOK * PACK],
+                )
+
+        def product(i, codes, sc, g, tag):
+            bank = psum.tile([P, PACK, TOK], F32, tag=tag, name=tag, bufs={"a": 3, "b": 1, "m": 2}[tag])
+            cols = slice(g * TOK, (g + 1) * TOK)
+            for t in range(PACK):
+                nc.tensor.matmul_mx(
+                    out=bank[:, t, :],
+                    lhsT=words[i][:, t * 256 : (t + 1) * 256].bitcast(FP4X4),
+                    lhsT_scale=scales[i][:, t * 128 : (t + 1) * 128],
+                    rhs=codes[:, cols].bitcast(FP8X4),
+                    rhs_scale=sc[:, cols],
+                    start=True,
+                    stop=True,
+                )
+            return bank
+
+        def make_a(c, g):
+            a_ps[c, g] = product(0, xq[c], xs[c], g, "a")
+
+        def make_b(c, g, tag="b"):
+            bank = product(1, xq[c], xs[c], g, tag)
+            t = work.tile([P, TOK, PACK], F32, name=f"b{g}")
+            bs[c, g] = t
+            nc.scalar.copy(out=t[:], in_=bank[:].rearrange("p t n -> p n t"))
+
+        prod = {}
+
+        def cross(c, i, j):
+            t = work.tile([P, TOK, PACK], F32, name=f"prod{i}{j}")
+            prod[c, i, j] = t
+            nc.vector.tensor_tensor(
+                out=t[:], in0=a_ps[c, i][:].rearrange("p t n -> p n t"), in1=bs[c, j][:], op=ALU.mult
+            )
+
+        def bracket(c, k, engine):
+            if c not in z:
+                tl = work.tile([P, G, TOK * PACK], BF16, name="z", align_bytes=64)
+                z[c] = tl
+            i, j = (k + 1) % 3, (k + 2) % 3
+            engine.tensor_tensor(
+                out=z[c][:, k, :],
+                in0=prod[c, i, j][:].rearrange("p n t -> p (n t)"),
+                in1=prod[c, j, i][:].rearrange("p n t -> p (n t)"),
+                op=ALU.subtract,
+            )
+
+        def quant_z(c, lo, hi):
+            if c not in zq:
+                t1 = work.tile([P, G * TOK], U32, name="zq", align_bytes=64)
+                t2 = work.tile([P, G * TOK], U8, name="zs", align_bytes=64)
+                zq[c], zs[c] = t1, t2
+            nc.vector.quantize_mx(
+                out=zq[c][:, lo * TOK : hi * TOK].bitcast(FP8X4),
+                scales=zs[c][:, lo * TOK : hi * TOK],
+                in_=z[c][:, lo:hi, :].rearrange("p g x -> p (g x)"),
+            )
+
+        def make_m(c, k, tag="m"):
+            m_ps[c, k] = product(2, zq[c], zs[c], k, tag)
+
+        def residual(c, k):
+            if c not in yt:
+                t1 = work.tile([P, G, PACK, TOK], F32, name="yt")
+                t2 = work.tile([P, G, TOK, PACK], BF16, name="y16", align_bytes=64)
+                yt[c], y16[c] = t1, t2
+            xv = xt[c][:].rearrange("p (g n t) -> p g n t", g=G, t=PACK)
+            for t in range(PACK):
+                nc.vector.scalar_tensor_tensor(
+                    out=yt[c][:, k, t, :], in0=xv[:, k, :, t], scalar=r_col[:, t : t + 1],
+                    in1=m_ps[c, k][:, t, :], op0=ALU.mult, op1=ALU.add,
+                )
+
+        def round_y(c, k, where):
+            src = yt[c][:, k].rearrange("p t n -> p n t")
+            if where == "scalar":
+                nc.scalar.copy(out=y16[c][:, k], in_=src)
+            elif where == "vector":
+                nc.vector.tensor_copy(out=y16[c][:, k], in_=src)
+            else:
+                nc.gpsimd.tensor_scalar(out=y16[c][:, k], in0=src, scalar1=1.0, scalar2=1.0, op0=ALU.mult, op1=ALU.mult)
+
+        def turn_y(c, k, where="scalar"):
+            bank = psum.tile([P, PACK, P], F32, tag="turn", name="turn_y")
+            for t in range(PACK):
+                nc.tensor.transpose(bank[:, t, :], yt[c][:, k, t, :], ident[:])
+            rows = work.tile([TOK, P, PACK], F32, name="rows", bufs=4)
+            src = bank[:].rearrange("n t p -> n p t")
+            if where == "scalar":
+                nc.scalar.copy(out=rows[:], in_=src)
+            else:
+                nc.vector.tensor_copy(out=rows[:], in_=src)
+            nc.sync.dma_start(out=out_0[k, c * TOK : (c + 1) * TOK, :], in_=rows[:].rearrange("n p t -> n (p t)"))
+
+        def quant_y(c, ks=(2, 1, 0)):
+            if c not in yq:
+                codes = work.tile([P, G, TOK], U32, name="yq", align_bytes=64)
+                yq[c] = codes
+            for k in ks:
+                nc.vector.quantize_mx(
+                    out=yq[c][:, k, :].bitcast(FP8X4),
+                    scales=y_scales_tail[:, k, :] if c == CHUNKS - 1 else y_scales_body[:, k, c * TOK : (c + 1) * TOK],
+                    in_=y16[c][:, k].rearrange("p n t -> p (n t)"),
+                )
+
+        def store_words(c, lo=0, hi=G):
+            nc.sync.dma_start(out=out_words[:, lo:hi, c * TOK : (c + 1) * TOK], in_=yq[c][:, lo:hi, :].bitcast(I32))
+
+        def store_scales(tl, c0, c1):
+            view = tl[:].rearrange("p g n -> p (g n)").bitcast(I32).rearrange("p (g n) -> p g n", g=G)
+            cols = slice(c0 * TOK // 4, c1 * TOK // 4)
+            for q in range(4):
+                nc.sync.dma_start(out=out_scales[4 * q : 4 * q + 4, :, cols], in_=view[32 * q : 32 * q + 4])
+
+        ctx.enter_context(tc.manual_schedule())
+
+        load_x(0)
+        for i in (1, 0, 2):
+            nc.vector.memset(raw_scales[i][:].bitcast(I32), 0)
+        load_words(1, v_words)
+        load_scales(1, v_scales, nc.scalar)
+        load_words(0, u_words)
+        load_x(1)
+        load_scales(0, u_scales, nc.scalar)
+        make_identity(nc, ident[:])
+        nc.gpsimd.dma_start(out=r_bf[:], in_=r.rearrange("(p t) -> p t", t=PACK))
+        load_scales(2, w_scales, nc.gpsimd)
+        nc.gpsimd.tensor_copy(out=r_col[:], in_=r_bf[:])
+        load_words(2, w_words)
+        load_x(2)
+        load_x(3)
+
+        turn_x(0)
+        turn_x(1)
+        permute_words(1)
+        permute_scales(1)
+        quant_x(0)
+        permute_words(0)
+        permute_scales(0)
+        make_b(0, 1)
+        make_b(0, 0, "m")
+        make_a(0, 0)
+        make_a(0, 1)
+        make_b(0, 2, "m")
+        make_a(0, 2)
+        quant_x(1)
+        permute_words(2)
+
+        last = CHUNKS - 1
+        for c in range(CHUNKS):
+            edge = c in (0, last)
+            cross(c, 0, 1)
+            cross(c, 1, 0)
+            bracket(c, 2, nc.gpsimd)
+            if c < last:
+                make_b(c + 1, 1)
+                make_b(c + 1, 0)
+            if c + 2 < CHUNKS:
+                turn_x(c + 2)
+            cross(c, 0, 2)
+            cross(c, 2, 0)
+            bracket(c, 1, nc.gpsimd)
+            if c < last:
+                make_a(c + 1, 0)
+                make_b(c + 1, 2)
+            cross(c, 1, 2)
+            cross(c, 2, 1)
+            bracket(c, 0, nc.vector if edge else nc.gpsimd)
+            if c < last:
+                make_a(c + 1, 1)
+                make_a(c + 1, 2)
+            if c == 0:
+                permute_scales(2)
+            if c == last:
+                quant_z(c, 1, 3)
+                quant_z(c, 0, 1)
+            if c > 0:
+                for k in (2, 1, 0):
+                    residual(c - 1, k)
+                    if k == 2:
+                        make_m(c - 1, 0)
+                        if c == last:
+                            for j in (2, 1, 0):
+                                make_m(c, j, "a")
+                    round_y(c - 1, k, "gpsimd" if c == last and k < 2 else "scalar")
+                    turn_y(c - 1, k)
+            if c < last:
+                quant_z(c, 1, 3)
+                quant_z(c, 0, 1)
+                make_m(c, 2)
+                make_m(c, 1)
+            if c + 2 < CHUNKS:
+                quant_x(c + 2)
+            if c > 1:
+                quant_y(c - 2)
+                store_words(c - 2)
+        for k in (2, 1, 0):
+            residual(last, k)
+            round_y(last, k, "gpsimd" if k else "vector")
+            turn_y(last, k)
+            if k == 1:
+                quant_y(last - 1)
+                store_words(last - 1)
+                store_scales(y_scales_body, 0, last)
+        quant_y(last, (2, 1))
+        store_words(last, 1, 3)
+        quant_y(last, (0,))
+        store_words(last, 0, 1)
+        store_scales(y_scales_tail, last, CHUNKS)

@@ -71,34 +71,36 @@ def tile_so3liebracketchannelmixer_x2_kernel(
                 in_=raw_scales[i][:].rearrange("p (m t) -> p t m", t=PACK),
             )
 
-        def turn_x(c):
+        def turn_x(c, parts=((0, 2), (2, 3))):
             rows = x_rows[c][:].rearrange("n g c -> n (g c)").bitcast(F32)
             dst = xt[c][:].bitcast(F32)
-            for g0, gn in ((0, 2), (2, 1)):
-                bank = psum.tile([P, 2, 2, TOK], F32, tag="turn", name="turn_x")
-                for g in range(gn):
+            for lo, hi in parts:
+                bank = psum.tile([P, 2, 2, TOK], F32, tag="turn", name="turn_x", bufs=2)
+                for g in range(lo, hi):
                     for h in range(2):
-                        lo = (g0 + g) * (C // 2)
-                        nc.tensor.transpose(bank[:, g, h, :], rows[:, lo + h : lo + C // 2 : 2], ident[:])
+                        nc.tensor.transpose(
+                            bank[:, g - lo, h, :], rows[:, g * C // 2 + h : (g + 1) * C // 2 : 2], ident[:]
+                        )
                 w = 2 * TOK
                 nc.scalar.copy(
-                    out=dst[:, g0 * w : (g0 + gn) * w].rearrange("p (g n h) -> p g n h", g=gn, h=2),
-                    in_=bank[:, 0:gn].rearrange("p g h n -> p g n h"),
+                    out=dst[:, lo * w : hi * w].rearrange("p (g n h) -> p g n h", g=hi - lo, h=2),
+                    in_=bank[:, 0 : hi - lo].rearrange("p g h n -> p g n h"),
                 )
 
-        def quant_x(c):
-            codes = work.tile([P, G * TOK], U32, name="xq", align_bytes=64)
-            sc = work.tile([P, G * TOK], U8, name="xs", align_bytes=64)
-            xq[c], xs[c] = codes, sc
-            for lo, hi in ((0, 2), (2, 3)):
+        def quant_x(c, parts=((0, 2), (2, 3))):
+            if c not in xq:
+                codes = work.tile([P, G * TOK], U32, name="xq", align_bytes=64)
+                sc = work.tile([P, G * TOK], U8, name="xs", align_bytes=64)
+                xq[c], xs[c] = codes, sc
+            for lo, hi in parts:
                 nc.vector.quantize_mx(
-                    out=codes[:, lo * TOK : hi * TOK].bitcast(FP8X4),
-                    scales=sc[:, lo * TOK : hi * TOK],
+                    out=xq[c][:, lo * TOK : hi * TOK].bitcast(FP8X4),
+                    scales=xs[c][:, lo * TOK : hi * TOK],
                     in_=xt[c][:, lo * TOK * PACK : hi * TOK * PACK],
                 )
 
         def product(i, codes, sc, g, tag):
-            bank = psum.tile([P, PACK, TOK], F32, tag=tag, name=tag, bufs={"a": 3, "b": 1, "m": 2}[tag])
+            bank = psum.tile([P, PACK, TOK], F32, tag=tag, name=tag, bufs={"a": 2, "b": 1, "m": 3}[tag])
             cols = slice(g * TOK, (g + 1) * TOK)
             for t in range(PACK):
                 nc.tensor.matmul_mx(
@@ -122,6 +124,18 @@ def tile_so3liebracketchannelmixer_x2_kernel(
             nc.scalar.copy(out=t[:], in_=bank[:].rearrange("p t n -> p n t"))
 
         prod = {}
+
+        a_sb = {}
+
+        def copy_a(c, i):
+            t = work.tile([P, TOK, PACK], F32, name="a_sb")
+            a_sb[c, i] = t
+            nc.scalar.copy(out=t[:], in_=a_ps[c, i][:].rearrange("p t n -> p n t"))
+
+        def cross_g(c, i, j):
+            t = work.tile([P, TOK, PACK], F32, name=f"prod{i}{j}")
+            prod[c, i, j] = t
+            nc.gpsimd.tensor_tensor(out=t[:], in0=a_sb[c, i][:], in1=bs[c, j][:], op=ALU.mult)
 
         def cross(c, i, j):
             t = work.tile([P, TOK, PACK], F32, name=f"prod{i}{j}")
@@ -178,7 +192,7 @@ def tile_so3liebracketchannelmixer_x2_kernel(
                 nc.gpsimd.tensor_scalar(out=y16[c][:, k], in0=src, scalar1=1.0, scalar2=1.0, op0=ALU.mult, op1=ALU.mult)
 
         def turn_y(c, k, where="scalar"):
-            bank = psum.tile([P, PACK, P], F32, tag="turn", name="turn_y")
+            bank = psum.tile([P, PACK, P], F32, tag="turn", name="turn_y", bufs=2)
             for t in range(PACK):
                 nc.tensor.transpose(bank[:, t, :], yt[c][:, k, t, :], ident[:])
             rows = work.tile([TOK, P, PACK], F32, name="rows", bufs=4)
@@ -217,88 +231,120 @@ def tile_so3liebracketchannelmixer_x2_kernel(
         load_words(1, v_words)
         load_scales(1, v_scales, nc.scalar)
         load_words(0, u_words)
-        load_x(1)
-        load_scales(0, u_scales, nc.scalar)
+        load_scales(0, u_scales, nc.sync)
         make_identity(nc, ident[:])
         nc.gpsimd.dma_start(out=r_bf[:], in_=r.rearrange("(p t) -> p t", t=PACK))
         load_scales(2, w_scales, nc.gpsimd)
         nc.gpsimd.tensor_copy(out=r_col[:], in_=r_bf[:])
+        load_x(1)
         load_words(2, w_words)
         load_x(2)
         load_x(3)
 
-        turn_x(0)
-        turn_x(1)
+        turn_x(0, ((1, 2), (0, 1)))
+        turn_x(0, ((2, 3),))
         permute_words(1)
         permute_scales(1)
-        quant_x(0)
+        quant_x(0, ((1, 2), (0, 1), (2, 3)))
         permute_words(0)
         permute_scales(0)
         make_b(0, 1)
-        make_b(0, 0, "m")
-        make_a(0, 0)
-        make_a(0, 1)
         make_b(0, 2, "m")
-        make_a(0, 2)
-        quant_x(1)
+        make_a(0, 0)
+        make_b(0, 0, "m")
+        make_a(0, 1)
+        turn_x(1)
         permute_words(2)
 
         last = CHUNKS - 1
-        for c in range(CHUNKS):
-            edge = c in (0, last)
+
+        def finish(c, k, rounder, copier):
+            residual(c, k)
+            round_y(c, k, rounder)
+            turn_y(c, k, copier)
+
+        cross(0, 0, 1)
+        cross(0, 0, 2)
+        make_a(0, 2)
+        turn_x(2)
+        cross(0, 1, 0)
+        bracket(0, 2, nc.gpsimd)
+        cross(0, 1, 2)
+        cross(0, 2, 0)
+        bracket(0, 1, nc.gpsimd)
+        cross(0, 2, 1)
+        quant_x(1)
+        bracket(0, 0, nc.vector)
+        make_b(1, 1)
+        make_b(1, 2, "m")
+        make_a(1, 0)
+        make_b(1, 0, "m")
+        make_a(1, 1)
+        permute_scales(2)
+        quant_z(0, 1, 3)
+        quant_z(0, 0, 1)
+        quant_x(2)
+
+        for c in range(1, last):
+            make_m(c - 1, 2)
             cross(c, 0, 1)
-            cross(c, 1, 0)
-            bracket(c, 2, nc.gpsimd)
-            if c < last:
-                make_b(c + 1, 1)
-                make_b(c + 1, 0)
+            cross(c, 0, 2)
+            make_a(c, 2)
+            make_m(c - 1, 1)
+            make_m(c - 1, 0)
+            make_b(c + 1, 1)
+            make_b(c + 1, 2)
             if c + 2 < CHUNKS:
                 turn_x(c + 2)
-            cross(c, 0, 2)
+            cross(c, 1, 0)
+            bracket(c, 2, nc.gpsimd)
+            cross(c, 1, 2)
+            make_a(c + 1, 0)
+            make_b(c + 1, 0)
             cross(c, 2, 0)
             bracket(c, 1, nc.gpsimd)
-            if c < last:
-                make_a(c + 1, 0)
-                make_b(c + 1, 2)
-            cross(c, 1, 2)
             cross(c, 2, 1)
-            bracket(c, 0, nc.vector if edge else nc.gpsimd)
-            if c < last:
-                make_a(c + 1, 1)
-                make_a(c + 1, 2)
-            if c == 0:
-                permute_scales(2)
-            if c == last:
-                quant_z(c, 1, 3)
-                quant_z(c, 0, 1)
-            if c > 0:
-                for k in (2, 1, 0):
-                    residual(c - 1, k)
-                    if k == 2:
-                        make_m(c - 1, 0)
-                        if c == last:
-                            for j in (2, 1, 0):
-                                make_m(c, j, "a")
-                    round_y(c - 1, k, "gpsimd" if c == last and k < 2 else "scalar")
-                    turn_y(c - 1, k)
-            if c < last:
-                quant_z(c, 1, 3)
-                quant_z(c, 0, 1)
-                make_m(c, 2)
-                make_m(c, 1)
+            bracket(c, 0, nc.gpsimd)
+            make_a(c + 1, 1)
+            for k in (2, 1, 0):
+                finish(c - 1, k, ["scalar","scalar","scalar"][2 - k], "scalar")
+            quant_z(c, 1, 3)
+            quant_z(c, 0, 1)
             if c + 2 < CHUNKS:
                 quant_x(c + 2)
             if c > 1:
                 quant_y(c - 2)
                 store_words(c - 2)
+
+        make_m(last - 1, 2)
+        cross(last, 0, 1)
+        cross(last, 0, 2)
+        make_a(last, 2)
+        make_m(last - 1, 1)
+        make_m(last - 1, 0)
+        cross(last, 1, 0)
+        bracket(last, 2, nc.gpsimd)
+        finish(last - 1, 2, ["scalar","scalar","gpsimd"][0], "scalar")
+        cross(last, 1, 2)
+        cross(last, 2, 0)
+        bracket(last, 1, nc.gpsimd)
+        finish(last - 1, 1, ["scalar","scalar","gpsimd"][1], "scalar")
+        finish(last - 1, 0, ["scalar","scalar","gpsimd"][2], "scalar")
+        cross(last, 2, 1)
+
+        quant_y(last - 2)
+        store_words(last - 2)
+        quant_z(last, 1, 3)
+        make_m(last, 2)
+        make_m(last, 1)
+        bracket(last, 0, nc.vector)
+        quant_z(last, 0, 1)
+        make_m(last, 0)
+        quant_y(last - 1)
+        store_words(last - 1)
+        store_scales(y_scales_body, 0, last)
         for k in (2, 1, 0):
-            residual(last, k)
-            round_y(last, k, "gpsimd" if k else "vector")
-            turn_y(last, k)
-            if k == 1:
-                quant_y(last - 1)
-                store_words(last - 1)
-                store_scales(y_scales_body, 0, last)
+            finish(last, k, ["gpsimd","gpsimd","vector"][2 - k], ["scalar","scalar","scalar"][2 - k])
         quant_y(last, (2, 1))
         store_words(last, 1, 3)
         quant_y(last, (0,))

@@ -52,9 +52,9 @@ def tile_so3liebracketchannelmixer_x2_kernel(
         def load_words(i, src):
             nc.sync.dma_start(out=raw_words[i][:].bitcast(I32), in_=src[0].bitcast(I32))
 
-        def load_scales(i, src, queue):
+        def load_scales(i, src, queues):
             for q in range(4):
-                queue.dma_start(
+                queues[q].dma_start(
                     out=raw_scales[i][32 * q : 32 * q + 4, :].bitcast(I32),
                     in_=src[0][4 * q : 4 * q + 4, :].bitcast(I32),
                 )
@@ -99,8 +99,9 @@ def tile_so3liebracketchannelmixer_x2_kernel(
                     in_=xt[c][:, lo * TOK * PACK : hi * TOK * PACK],
                 )
 
-        def product(i, codes, sc, g, tag):
+        def product(i, codes, sc, g, tag, src=0, busy=0):
             bank = psum.tile([P, PACK, TOK], F32, tag=tag, name=tag, bufs={"a": 2, "b": 1, "m": 3}[tag])
+            keep_busy(bank, src, busy)
             cols = slice(g * TOK, (g + 1) * TOK)
             for t in range(PACK):
                 nc.tensor.matmul_mx(
@@ -114,11 +115,23 @@ def tile_so3liebracketchannelmixer_x2_kernel(
                 )
             return bank
 
+        def keep_busy(bank, c, n):
+            for i in range(n):
+                nc.tensor.matmul_mx(
+                    out=bank[:].rearrange("p t n -> p (t n)"),
+                    lhsT=xq[c][:, 0:P].bitcast(FP8X4),
+                    lhsT_scale=xs[c][:, 0:P],
+                    rhs=words[0][:].bitcast(FP4X4),
+                    rhs_scale=scales[0][:],
+                    start=True,
+                    stop=True,
+                )
+
         def make_a(c, g):
             a_ps[c, g] = product(0, xq[c], xs[c], g, "a")
 
-        def make_b(c, g, tag="b"):
-            bank = product(1, xq[c], xs[c], g, tag)
+        def make_b(c, g, tag="b", src=0, busy=0):
+            bank = product(1, xq[c], xs[c], g, tag, src, busy)
             t = work.tile([P, TOK, PACK], F32, name=f"b{g}")
             bs[c, g] = t
             nc.scalar.copy(out=t[:], in_=bank[:].rearrange("p t n -> p n t"))
@@ -167,8 +180,8 @@ def tile_so3liebracketchannelmixer_x2_kernel(
                 in_=z[c][:, lo:hi, :].rearrange("p g x -> p (g x)"),
             )
 
-        def make_m(c, k, tag="m"):
-            m_ps[c, k] = product(2, zq[c], zs[c], k, tag)
+        def make_m(c, k, tag="m", src=0, busy=0):
+            m_ps[c, k] = product(2, zq[c], zs[c], k, tag, src, busy)
 
         def residual(c, k):
             if c not in yt:
@@ -229,14 +242,14 @@ def tile_so3liebracketchannelmixer_x2_kernel(
         for i in (1, 0, 2):
             nc.vector.memset(raw_scales[i][:].bitcast(I32), 0)
         load_words(1, v_words)
-        load_scales(1, v_scales, nc.scalar)
+        load_scales(1, v_scales, [nc.scalar] * 4)
         load_words(0, u_words)
-        load_scales(0, u_scales, nc.sync)
+        load_x(1)
+        load_scales(0, u_scales, [nc.sync] * 4)
         make_identity(nc, ident[:])
         nc.gpsimd.dma_start(out=r_bf[:], in_=r.rearrange("(p t) -> p t", t=PACK))
-        load_scales(2, w_scales, nc.gpsimd)
+        load_scales(2, w_scales, [nc.gpsimd] * 4)
         nc.gpsimd.tensor_copy(out=r_col[:], in_=r_bf[:])
-        load_x(1)
         load_words(2, w_words)
         load_x(2)
         load_x(3)
@@ -245,8 +258,10 @@ def tile_so3liebracketchannelmixer_x2_kernel(
         turn_x(0, ((2, 3),))
         permute_words(1)
         permute_scales(1)
-        quant_x(0, ((1, 2), (0, 1), (2, 3)))
+        quant_x(0, ((1, 2),))
         permute_words(0)
+        quant_x(0, ((0, 1),))
+        quant_x(0, ((2, 3),))
         permute_scales(0)
         make_b(0, 1)
         make_b(0, 2, "m")
@@ -271,13 +286,13 @@ def tile_so3liebracketchannelmixer_x2_kernel(
         bracket(0, 2, nc.gpsimd)
         cross(0, 1, 2)
         cross(0, 2, 0)
-        bracket(0, 1, nc.gpsimd)
         cross(0, 2, 1)
+        bracket(0, 1, nc.vector)
         quant_x(1)
         bracket(0, 0, nc.vector)
         make_b(1, 1)
-        make_b(1, 2, "m")
         make_a(1, 0)
+        make_b(1, 2, "m")
         make_b(1, 0, "m")
         make_a(1, 1)
         permute_scales(2)
@@ -293,6 +308,9 @@ def tile_so3liebracketchannelmixer_x2_kernel(
             make_m(c - 1, 1)
             make_m(c - 1, 0)
             make_b(c + 1, 1)
+            if c > 1:
+                round_y(c - 2, 0, "scalar")
+                turn_y(c - 2, 0)
             make_b(c + 1, 2)
             if c + 2 < CHUNKS:
                 turn_x(c + 2)
@@ -306,8 +324,9 @@ def tile_so3liebracketchannelmixer_x2_kernel(
             cross(c, 2, 1)
             bracket(c, 0, nc.gpsimd)
             make_a(c + 1, 1)
-            for k in (2, 1, 0):
-                finish(c - 1, k, ["scalar","scalar","scalar"][2 - k], "scalar")
+            finish(c - 1, 2, "scalar", "scalar")
+            finish(c - 1, 1, "scalar", "scalar")
+            residual(c - 1, 0)
             quant_z(c, 1, 3)
             quant_z(c, 0, 1)
             if c + 2 < CHUNKS:
@@ -322,6 +341,8 @@ def tile_so3liebracketchannelmixer_x2_kernel(
         make_a(last, 2)
         make_m(last - 1, 1)
         make_m(last - 1, 0)
+        round_y(last - 2, 0, "scalar")
+        turn_y(last - 2, 0)
         cross(last, 1, 0)
         bracket(last, 2, nc.gpsimd)
         finish(last - 1, 2, ["scalar","scalar","gpsimd"][0], "scalar")

from contextlib import ExitStack

import concourse.mybir as mybir
from concourse.masks import make_identity

F32 = mybir.dt.float32
BF16 = mybir.dt.bfloat16
I32 = mybir.dt.int32
U32 = mybir.dt.uint32
U8 = mybir.dt.uint8
FP8X4 = mybir.dt.float8_e4m3fn_x4
FP4X4 = mybir.dt.float4_e2m1fn_x4
ALU = mybir.AluOpType

G, N, C = 3, 512, 512
P = 128
PACK = 4
TOK = 128
CHUNKS = N // TOK
FLOPS = 2 * 3 * G * N * C * C


def tile_so3liebracketchannelmixer_x2_kernel(
    tc, x, u_words, u_scales, v_words, v_scales, w_words, w_scales, r, out_0, out_1, out_2
):
    nc = tc.nc
    with ExitStack() as ctx:
        keep = ctx.enter_context(tc.tile_pool(name="keep", bufs=1))
        work = ctx.enter_context(tc.tile_pool(name="work", bufs=2))
        psum = ctx.enter_context(tc.psum_pool(name="psum", bufs=2))

        out_words = out_1[0].rearrange("p m t -> p (m t)").bitcast(I32).rearrange("p (g m) -> p g m", g=G)
        out_scales = out_2[0].bitcast(I32).rearrange("q (g m) -> q g m", g=G)

        raw_words = [keep.tile([P, 2 * C], U8, name=f"raw_words{i}", align_bytes=64) for i in range(3)]
        raw_scales = [keep.tile([P, C], U8, name=f"raw_scales{i}", align_bytes=64) for i in range(3)]
        words = [keep.tile([P, 2 * C], U8, name=f"words{i}", align_bytes=64) for i in range(3)]
        scales = [keep.tile([P, C], U8, name=f"scales{i}", align_bytes=64) for i in range(3)]
        x_rows = [keep.tile([TOK, G, C], BF16, name=f"x_rows{c}", align_bytes=64) for c in range(CHUNKS)]
        xt = [keep.tile([P, G * TOK * PACK], BF16, name=f"xt{c}", align_bytes=64) for c in range(CHUNKS)]
        ident = keep.tile([P, P], F32, name="ident")
        r_bf = keep.tile([P, PACK], BF16, name="r_bf")
        r_col = keep.tile([P, PACK], F32, name="r_col")
        y_scales_body = keep.tile([P, G, N - TOK], U8, name="y_scales_body", align_bytes=64)
        y_scales_tail = keep.tile([P, G, TOK], U8, name="y_scales_tail", align_bytes=64)

        xq, xs, bs, z, zq, zs, yt, y16, yq, m_ps, a_ps = {}, {}, {}, {}, {}, {}, {}, {}, {}, {}, {}

        def load_x(c):
            nc.sync.dma_start(out=x_rows[c][:], in_=x[:, c * TOK : (c + 1) * TOK, :].rearrange("g n c -> n g c"))

        def load_words(i, src):
            nc.sync.dma_start(out=raw_words[i][:].bitcast(I32), in_=src[0].bitcast(I32))

        def load_scales(i, src, queues):
            for q in range(4):
                queues[q].dma_start(
                    out=raw_scales[i][32 * q : 32 * q + 4, :].bitcast(I32),
                    in_=src[0][4 * q : 4 * q + 4, :].bitcast(I32),
                )

        def permute_words(i):
            nc.vector.tensor_copy(
                out=words[i][:].rearrange("p (t m b) -> p t m b", t=PACK, b=2),
                in_=raw_words[i][:].rearrange("p (m t b) -> p t m b", t=PACK, b=2),
            )

        def permute_scales(i):
            nc.vector.tensor_copy(
                out=scales[i][:].rearrange("p (t m) -> p t m", t=PACK),
                in_=raw_scales[i][:].rearrange("p (m t) -> p t m", t=PACK),
            )

        def turn_x(c, parts=((0, 2), (2, 3))):
            rows = x_rows[c][:].rearrange("n g c -> n (g c)").bitcast(F32)
            dst = xt[c][:].bitcast(F32)
            for lo, hi in parts:
                bank = psum.tile([P, 2, 2, TOK], F32, tag="turn", name="turn_x", bufs=2)
                for g in range(lo, hi):
                    for h in range(2):
                        nc.tensor.transpose(
                            bank[:, g - lo, h, :], rows[:, g * C // 2 + h : (g + 1) * C // 2 : 2], ident[:]
                        )
                w = 2 * TOK
                nc.scalar.copy(
                    out=dst[:, lo * w : hi * w].rearrange("p (g n h) -> p g n h", g=hi - lo, h=2),
                    in_=bank[:, 0 : hi - lo].rearrange("p g h n -> p g n h"),
                )

        def quant_x(c, parts=((0, 2), (2, 3))):
            if c not in xq:
                codes = work.tile([P, G * TOK], U32, name="xq", align_bytes=64)
                sc = work.tile([P, G * TOK], U8, name="xs", align_bytes=64)
                xq[c], xs[c] = codes, sc
            for lo, hi in parts:
                nc.vector.quantize_mx(
                    out=xq[c][:, lo * TOK : hi * TOK].bitcast(FP8X4),
                    scales=xs[c][:, lo * TOK : hi * TOK],
                    in_=xt[c][:, lo * TOK * PACK : hi * TOK * PACK],
                )

        def product(i, codes, sc, g, tag, src=0, busy=0):
            bank = psum.tile([P, PACK, TOK], F32, tag=tag, name=tag, bufs={"a": 2, "b": 1, "m": 3}[tag])
            keep_busy(bank, src, busy)
            cols = slice(g * TOK, (g + 1) * TOK)
            for t in range(PACK):
                nc.tensor.matmul_mx(
                    out=bank[:, t, :],
                    lhsT=words[i][:, t * 256 : (t + 1) * 256].bitcast(FP4X4),
                    lhsT_scale=scales[i][:, t * 128 : (t + 1) * 128],
                    rhs=codes[:, cols].bitcast(FP8X4),
                    rhs_scale=sc[:, cols],
                    start=True,
                    stop=True,
                )
            return bank

        def keep_busy(bank, c, n):
            for i in range(n):
                nc.tensor.matmul_mx(
                    out=bank[:].rearrange("p t n -> p (t n)"),
                    lhsT=xq[c][:, 0:P].bitcast(FP8X4),
                    lhsT_scale=xs[c][:, 0:P],
                    rhs=words[0][:].bitcast(FP4X4),
                    rhs_scale=scales[0][:],
                    start=True,
                    stop=True,
                )

        def make_a(c, g):
            a_ps[c, g] = product(0, xq[c], xs[c], g, "a")

        def make_b(c, g, tag="b", src=0, busy=0):
            bank = product(1, xq[c], xs[c], g, tag, src, busy)
            t = work.tile([P, TOK, PACK], F32, name=f"b{g}")
            bs[c, g] = t
            nc.scalar.copy(out=t[:], in_=bank[:].rearrange("p t n -> p n t"))

        prod = {}

        a_sb = {}

        def copy_a(c, i):
            t = work.tile([P, TOK, PACK], F32, name="a_sb")
            a_sb[c, i] = t
            nc.scalar.copy(out=t[:], in_=a_ps[c, i][:].rearrange("p t n -> p n t"))

        def cross_g(c, i, j):
            t = work.tile([P, TOK, PACK], F32, name=f"prod{i}{j}")
            prod[c, i, j] = t
            nc.gpsimd.tensor_tensor(out=t[:], in0=a_sb[c, i][:], in1=bs[c, j][:], op=ALU.mult)

        def cross(c, i, j):
            t = work.tile([P, TOK, PACK], F32, name=f"prod{i}{j}")
            prod[c, i, j] = t
            nc.vector.tensor_tensor(
                out=t[:], in0=a_ps[c, i][:].rearrange("p t n -> p n t"), in1=bs[c, j][:], op=ALU.mult
            )

        def bracket(c, k, engine):
            if c not in z:
                tl = work.tile([P, G, TOK * PACK], BF16, name="z", align_bytes=64)
                z[c] = tl
            i, j = (k + 1) % 3, (k + 2) % 3
            engine.tensor_tensor(
                out=z[c][:, k, :],
                in0=prod[c, i, j][:].rearrange("p n t -> p (n t)"),
                in1=prod[c, j, i][:].rearrange("p n t -> p (n t)"),
                op=ALU.subtract,
            )

        def quant_z(c, lo, hi):
            if c not in zq:
                t1 = work.tile([P, G * TOK], U32, name="zq", align_bytes=64)
                t2 = work.tile([P, G * TOK], U8, name="zs", align_bytes=64)
                zq[c], zs[c] = t1, t2
            nc.vector.quantize_mx(
                out=zq[c][:, lo * TOK : hi * TOK].bitcast(FP8X4),
                scales=zs[c][:, lo * TOK : hi * TOK],
                in_=z[c][:, lo:hi, :].rearrange("p g x -> p (g x)"),
            )

        def make_m(c, k, tag="m", src=0, busy=0):
            m_ps[c, k] = product(2, zq[c], zs[c], k, tag, src, busy)

        def residual(c, k):
            if c not in yt:
                t1 = work.tile([P, G, PACK, TOK], F32, name="yt")
                t2 = work.tile([P, G, TOK, PACK], BF16, name="y16", align_bytes=64)
                yt[c], y16[c] = t1, t2
            xv = xt[c][:].rearrange("p (g n t) -> p g n t", g=G, t=PACK)
            for t in range(PACK):
                nc.vector.scalar_tensor_tensor(
                    out=yt[c][:, k, t, :], in0=xv[:, k, :, t], scalar=r_col[:, t : t + 1],
                    in1=m_ps[c, k][:, t, :], op0=ALU.mult, op1=ALU.add,
                )

        def round_y(c, k, where):
            src = yt[c][:, k].rearrange("p t n -> p n t")
            if where == "scalar":
                nc.scalar.copy(out=y16[c][:, k], in_=src)
            elif where == "vector":
                nc.vector.tensor_copy(out=y16[c][:, k], in_=src)
            else:
                nc.gpsimd.tensor_scalar(out=y16[c][:, k], in0=src, scalar1=1.0, scalar2=1.0, op0=ALU.mult, op1=ALU.mult)

        def turn_y(c, k, where="scalar"):
            bank = psum.tile([P, PACK, P], F32, tag="turn", name="turn_y", bufs=2)
            for t in range(PACK):
                nc.tensor.transpose(bank[:, t, :], yt[c][:, k, t, :], ident[:])
            rows = work.tile([TOK, P, PACK], F32, name="rows", bufs=4)
            src = bank[:].rearrange("n t p -> n p t")
            if where == "scalar":
                nc.scalar.copy(out=rows[:], in_=src)
            else:
                nc.vector.tensor_copy(out=rows[:], in_=src)
            nc.sync.dma_start(out=out_0[k, c * TOK : (c + 1) * TOK, :], in_=rows[:].rearrange("n p t -> n (p t)"))

        def quant_y(c, ks=(2, 1, 0)):
            if c not in yq:
                codes = work.tile([P, G, TOK], U32, name="yq", align_bytes=64)
                yq[c] = codes
            for k in ks:
                nc.vector.quantize_mx(
                    out=yq[c][:, k, :].bitcast(FP8X4),
                    scales=y_scales_tail[:, k, :] if c == CHUNKS - 1 else y_scales_body[:, k, c * TOK : (c + 1) * TOK],
                    in_=y16[c][:, k].rearrange("p n t -> p (n t)"),
                )

        def store_words(c, lo=0, hi=G):
            nc.sync.dma_start(out=out_words[:, lo:hi, c * TOK : (c + 1) * TOK], in_=yq[c][:, lo:hi, :].bitcast(I32))

        def store_scales(tl, c0, c1):
            view = tl[:].rearrange("p g n -> p (g n)").bitcast(I32).rearrange("p (g n) -> p g n", g=G)
            cols = slice(c0 * TOK // 4, c1 * TOK // 4)
            for q in range(4):
                nc.sync.dma_start(out=out_scales[4 * q : 4 * q + 4, :, cols], in_=view[32 * q : 32 * q + 4])

        ctx.enter_context(tc.manual_schedule())

        load_x(0)
        for i in (1, 0, 2):
            nc.vector.memset(raw_scales[i][:].bitcast(I32), 0)
        load_words(1, v_words)
        load_scales(1, v_scales, [nc.scalar] * 4)
        load_words(0, u_words)
        load_x(1)
        load_scales(0, u_scales, [nc.sync] * 4)
        make_identity(nc, ident[:])
        nc.gpsimd.dma_start(out=r_bf[:], in_=r.rearrange("(p t) -> p t", t=PACK))
        load_scales(2, w_scales, [nc.gpsimd] * 4)
        nc.gpsimd.tensor_copy(out=r_col[:], in_=r_bf[:])
        load_words(2, w_words)
        load_x(2)
        load_x(3)

        turn_x(0, ((1, 2), (0, 1)))
        turn_x(0, ((2, 3),))
        permute_words(1)
        permute_scales(1)
        quant_x(0, ((1, 2),))
        permute_words(0)
        quant_x(0, ((0, 1),))
        quant_x(0, ((2, 3),))
        permute_scales(0)
        make_b(0, 1)
        make_b(0, 2, "m")
        make_a(0, 0)
        make_b(0, 0, "m")
        make_a(0, 1)
        turn_x(1)
        permute_words(2)

        last = CHUNKS - 1

        def finish(c, k, rounder, copier):
            residual(c, k)
            round_y(c, k, rounder)
            turn_y(c, k, copier)

        cross(0, 0, 1)
        cross(0, 0, 2)
        make_a(0, 2)
        turn_x(2)
        cross(0, 1, 0)
        bracket(0, 2, nc.gpsimd)
        cross(0, 1, 2)
        cross(0, 2, 0)
        cross(0, 2, 1)
        bracket(0, 1, nc.vector)
        quant_x(1)
        bracket(0, 0, nc.vector)
        make_b(1, 1)
        make_a(1, 0)
        make_b(1, 2, "m")
        make_b(1, 0, "m")
        make_a(1, 1)
        permute_scales(2)
        quant_z(0, 1, 3)
        quant_z(0, 0, 1)
        quant_x(2)

        for c in range(1, last):
            make_m(c - 1, 2)
            cross(c, 0, 1)
            cross(c, 0, 2)
            make_a(c, 2)
            make_m(c - 1, 1)
            make_m(c - 1, 0)
            make_b(c + 1, 1)
            if c > 1:
                round_y(c - 2, 0, "scalar")
                turn_y(c - 2, 0)
            make_b(c + 1, 2)
            if c + 2 < CHUNKS:
                turn_x(c + 2)
            cross(c, 1, 0)
            bracket(c, 2, nc.gpsimd)
            cross(c, 1, 2)
            make_a(c + 1, 0)
            make_b(c + 1, 0)
            cross(c, 2, 0)
            bracket(c, 1, nc.gpsimd)
            cross(c, 2, 1)
            bracket(c, 0, nc.gpsimd)
            make_a(c + 1, 1)
            finish(c - 1, 2, "scalar", "scalar")
            finish(c - 1, 1, "scalar", "scalar")
            residual(c - 1, 0)
            quant_z(c, 1, 3)
            quant_z(c, 0, 1)
            if c + 2 < CHUNKS:
                quant_x(c + 2)
            if c > 1:
                quant_y(c - 2)
                store_words(c - 2)

        make_m(last - 1, 2)
        cross(last, 0, 1)
        cross(last, 0, 2)
        make_a(last, 2)
        make_m(last - 1, 1)
        make_m(last - 1, 0)
        round_y(last - 2, 0, "scalar")
        turn_y(last - 2, 0)
        cross(last, 1, 0)
        bracket(last, 2, nc.gpsimd)
        finish(last - 1, 2, ["scalar","scalar","gpsimd"][0], "scalar")
        cross(last, 1, 2)
        cross(last, 2, 0)
        bracket(last, 1, nc.gpsimd)
        finish(last - 1, 1, ["scalar","scalar","gpsimd"][1], "scalar")
        finish(last - 1, 0, ["scalar","scalar","gpsimd"][2], "scalar")
        cross(last, 2, 1)

        quant_y(last - 2)
        store_words(last - 2)
        quant_z(last, 1, 3)
        make_m(last, 2)
        make_m(last, 1)
        bracket(last, 0, nc.vector)
        quant_z(last, 0, 1)
        make_m(last, 0)
        quant_y(last - 1)
        store_words(last - 1)
        store_scales(y_scales_body, 0, last)
        for k in (2, 1, 0):
            finish(last, k, ["gpsimd","gpsimd","vector"][2 - k], ["scalar","scalar","scalar"][2 - k])
        quant_y(last, (2, 1))
        store_words(last, 1, 3)
        quant_y(last, (0,))
        store_words(last, 0, 1)
        store_scales(y_scales_tail, last, CHUNKS)
